import numpy as np
import ml_dtypes


def mxq(x, axis, fmt="e4m3"):
    dtype, down = {"e4m3": (ml_dtypes.float8_e4m3fn, 7), "e5m2": (ml_dtypes.float8_e5m2, 14)}[fmt]
    v = np.moveaxis(np.asarray(x, np.float32).astype(ml_dtypes.bfloat16).astype(np.float64), axis, -1)
    blocks = v.reshape(v.shape[:-1] + (-1, 32))
    amax = np.abs(blocks).max(-1, keepdims=True)
    byte = np.maximum(np.where(amax > 0, np.frexp(amax)[1] - 1 + 127, 0) - down, 1)
    scale = np.exp2(byte - 127.0)
    codes = (blocks / scale).astype(np.float32).astype(dtype).astype(np.float64)
    return np.moveaxis((codes * scale).reshape(v.shape), -1, axis)


WIDE = False


def mx_kscale(k):
    if not WIDE:
        return np.ones(k)
    levels = np.array([30, -30])
    if k % 512:
        return np.exp2(np.random.permutation(np.resize(levels, k // 32))).repeat(32)
    a = np.empty((k // 512, 16))
    for p in range(k // 512):
        a[p, :8] = np.random.permutation(np.resize(levels, 8))
        for g in range(8):
            far = levels[np.abs(levels - a[p, g]) >= 10]
            a[p, g + 8] = far[np.random.randint(len(far))]
    return np.exp2(a.ravel()).repeat(32)


def f64(x):
    return np.asarray(x).astype(np.float64)


def striped(idx):
    return np.tile(np.asarray(idx).reshape(-1, 16).T, (8, 1)).astype(np.uint16)


def unstriped(offs):
    return offs[:16].T.reshape(-1).astype(np.int64)


E2M1 = np.array([0.0, 0.5, 1.0, 1.5, 2.0, 3.0, 4.0, 6.0, -0.0, -0.5, -1.0, -1.5, -2.0, -3.0, -4.0, -6.0])


def pack_weight(w, fmt):
    k, n = w.shape
    w = f64(np.asarray(w, np.float32).astype(ml_dtypes.bfloat16)).reshape(k // 32, 32, n)
    amax = np.abs(w).max(1)
    if fmt == "e4m3":
        byte = np.frexp(amax)[1] - 1 + 127 - 7
    else:
        mant, ex = np.frexp(amax / 6.0)
        byte = np.where(mant > 0.5, ex, ex - 1) + 127
    byte = np.clip(np.where(amax > 0, byte, 1), 1, 254)
    scaled = (w * np.exp2(127.0 - byte)[:, None, :]).reshape(k, n).astype(np.float32)
    by_word = np.ascontiguousarray(scaled.reshape(k // 512, 128, 4, n).transpose(0, 1, 3, 2))
    if fmt == "e4m3":
        words = by_word.astype(ml_dtypes.float8_e4m3fn).view(np.uint8)
    else:
        c = by_word.astype(ml_dtypes.float4_e2m1fn).view(np.uint8) & 0xF
        words = (c[..., 0::2] | (c[..., 1::2] << 4)).reshape(k // 512, 128, 2 * n)
    return np.ascontiguousarray(words), np.ascontiguousarray(byte.astype(np.uint8).reshape(k // 512, 16, n))


def unpack_weight(words, scales, fmt):
    g, _, n = scales.shape
    words = np.ascontiguousarray(words).reshape(g, 128, n, -1)
    if fmt == "e4m3":
        vals = words.view(ml_dtypes.float8_e4m3fn).astype(np.float64)
    else:
        nib = np.empty((g, 128, n, 4), np.uint8)
        nib[..., 0::2] = words & 0xF
        nib[..., 1::2] = words >> 4
        vals = E2M1[nib]
    vals = vals * np.repeat(np.exp2(scales.astype(np.float64) - 127.0), 8, axis=1)[..., None]
    return vals.transpose(0, 1, 3, 2).reshape(g * 512, n)


def bf(x):
    return np.asarray(x, np.float32).astype(ml_dtypes.bfloat16)


def planes(Y):
    r, m = Y.shape
    b = f64(bf(Y)).reshape(r // 32, 32, m)
    amax = np.abs(b).max(1)
    byte = np.clip(np.where(amax > 0, np.frexp(amax)[1] - 1 + 127 - 7, 1), 1, 254)
    codes = (b * np.exp2(127.0 - byte)[:, None, :]).reshape(r, m).astype(np.float32).astype(ml_dtypes.float8_e4m3fn).view(np.uint8)
    words = codes.reshape(r // 512, 128, 4, m).transpose(0, 1, 3, 2)
    return np.ascontiguousarray(words), np.ascontiguousarray(byte.astype(np.uint8).reshape(r // 512, 16, m))


N, K, T, J = 512, 512, 2048, 512


def setup_inputs():
    n = np.random.standard_normal
    idx = np.random.permutation(T)[:J]
    idx2 = np.random.permutation(T)[:J]
    fn = mx_kscale(N)
    wp = pack_weight(n((N, K)) * 1 / np.sqrt(N) * fn[:, None], "e4m3")
    return {
        "g": (n((N, T)) * np.exp(0.5 * n((1, T))) / fn[:, None]).astype(np.float32),
        "rw": (np.random.uniform(0.5, 2.0, (1, J))).astype(np.float32),
        "w_words": wp[0],
        "w_scales": wp[1],
        "run": (0.5 * n((K, J))).astype(np.float32),
        "offs": striped(idx),
        "offs2": striped(idx2),
    }


def reference(g, rw, w_words, w_scales, run, offs, offs2):
    idx = unstriped(offs)
    idx2 = unstriped(offs2)
    wu = unpack_weight(w_words, w_scales, "e4m3")
    d = (f64(g)[:, idx] - f64(g)[:, idx2]) * f64(rw)
    dq = mxq(d, 0, "e5m2")
    p = wu.T @ dq
    y = p + f64(run)
    words, scales = planes(y)
    return y, words, scales

@@ -1,0 +1,177 @@
+from contextlib import ExitStack
+
+import concourse.mybir as mybir
+from concourse.masks import make_identity
+
+N, K, T, J = 512, 512, 2048, 512
+FLOPS = 2 * N * K * J
+
+F32 = mybir.dt.float32
+BF16 = mybir.dt.bfloat16
+I32 = mybir.dt.int32
+U32 = mybir.dt.uint32
+U16 = mybir.dt.uint16
+U8 = mybir.dt.uint8
+E4M3 = mybir.dt.float8_e4m3fn_x4
+E5M2 = mybir.dt.float8_e5m2_x4
+ALU = mybir.AluOpType
+COPY = mybir.ActivationFunctionType.Copy
+
+P = 128
+PACK = 4
+CHUNK = 128
+CHUNKS = J // CHUNK
+COLS = CHUNK // 16
+
+
+def tile_list_gradient_of_pair_gaps_pl_kernel(tc, g, rw, w_words, w_scales, run, offs, offs2, out_0, out_1, out_2):
+    nc = tc.nc
+    with ExitStack() as ctx:
+        keep = ctx.enter_context(tc.tile_pool(name="keep", bufs=1))
+        psum = ctx.enter_context(tc.psum_pool(name="psum", bufs=1))
+
+        first = keep.tile([P, J // 16], U16, name="first")
+        second = keep.tile([P, J // 16], U16, name="second")
+        planes = [keep.tile([P, T], F32, name=f"g{i}") for i in range(PACK)]
+        w_raw = keep.tile([P, K], U32, name="w_raw")
+        ws_raw = keep.tile([P, K], U8, name="ws_raw")
+        w_dealt = keep.tile([P, K], U32, name="w_dealt", align_bytes=64)
+        ws_dealt = keep.tile([P, K], U8, name="ws_dealt", align_bytes=64)
+        rw_cols = keep.tile([P, PACK], F32, name="rw_cols")
+        ident = keep.tile([P, P], F32, name="ident")
+        run_half = [keep.tile([P, PACK, 2 * CHUNK], F32, name=f"run{h}") for h in range(2)]
+
+        g_planes = g.rearrange("(p i) t -> i p t", i=PACK)
+        run_rows = run.rearrange("(p t) j -> p t j", t=PACK)
+        out_rows = out_0.rearrange("(p t) j -> p t j", t=PACK)
+
+        nc.sync.dma_start(out=w_raw[:].bitcast(I32), in_=w_words[0].rearrange("p n t -> p (n t)").bitcast(I32))
+        nc.sync.dma_start(out=planes[0][:], in_=g_planes[0])
+        nc.sync.dma_start(second[:], offs2)
+        nc.sync.dma_start(first[:], offs)
+        nc.sync.dma_start(out=rw_cols[:], in_=rw.rearrange("o (k c) -> k (o c)", c=PACK))
+        for i in range(1, PACK):
+            nc.sync.dma_start(out=planes[i][:], in_=g_planes[i])
+        for h in range(2):
+            nc.sync.dma_start(out=run_half[h][:], in_=run_rows[:, :, h * 2 * CHUNK : (h + 1) * 2 * CHUNK])
+
+        nc.vector.memset(ws_raw[:].bitcast(U32), 0)
+        make_identity(nc, ident[:])
+        for q in range(4):
+            nc.gpsimd.dma_start(
+                out=ws_raw[32 * q : 32 * q + 4, :].bitcast(I32),
+                in_=w_scales[0, 4 * q : 4 * q + 4, :].bitcast(I32),
+            )
+
+        nc.vector.tensor_copy(
+            out=w_dealt[:].rearrange("p (t m) -> p t m", t=PACK),
+            in_=w_raw[:].rearrange("p (m t) -> p t m", t=PACK),
+        )
+        nc.vector.tensor_copy(
+            out=ws_dealt[:].rearrange("p (t m) -> p t m", t=PACK),
+            in_=ws_raw[:].rearrange("p (m t) -> p t m", t=PACK),
+        )
+
+        rw_bank = psum.tile([P, PACK, P], F32, name="rw_bank")
+        for c in range(PACK):
+            nc.tensor.transpose(rw_bank[:, c, :], rw_cols[:, c : c + 1].to_broadcast([P, P]), ident[:])
+        rw_all = rw_bank[:].rearrange("p c k -> p k c")
+
+        pairs = [keep.tile([P, 2, J], BF16, name=f"pair{u}") for u in range(2)]
+        d_in = [keep.tile([P, CHUNK, PACK], BF16, name=f"d_in{c}", align_bytes=64) for c in range(CHUNKS)]
+
+        def pick_second(i, tag, j0, j1):
+            picked = keep.tile([P, j1 - j0], F32, name=f"picked{tag}")
+            nc.scalar.activation(picked[:], planes[i][:].indirect(second[:, j0 // 16 : j1 // 16]), COPY)
+            return picked
+
+        def subtract(i, tag, j0, j1, picked):
+            gap = keep.tile([P, j1 - j0], F32, name=f"gap{tag}")
+            nc.vector.tensor_tensor(gap[:], planes[i][:].indirect(first[:, j0 // 16 : j1 // 16]), picked[:], ALU.subtract)
+            return gap
+
+        def weigh(i, j0, j1, gap):
+            nc.vector.tensor_tensor(
+                out=pairs[i // 2][:, i % 2, j0:j1].rearrange("p (k c) -> p k c", c=PACK),
+                in0=gap[:].rearrange("p (k c) -> p k c", c=PACK),
+                in1=rw_all[:, j0 // PACK : j1 // PACK, :],
+                op=ALU.mult,
+            )
+
+        def weave_pair(u, c):
+            nc.scalar.copy(
+                out=d_in[c][:, :, 2 * u : 2 * u + 2],
+                in_=pairs[u][:, :, c * CHUNK : (c + 1) * CHUNK].rearrange("p e j -> p j e"),
+            )
+
+        for i in range(PACK - 1):
+            gap = subtract(i, f"_{i}", 0, J, pick_second(i, f"_{i}", 0, J))
+            weigh(i, 0, J, gap)
+            if i == 1:
+                for c in range(CHUNKS):
+                    weave_pair(0, c)
+
+        last = PACK - 1
+        d_codes = [keep.tile([P, CHUNK], U32, name=f"d_codes{c}", align_bytes=64) for c in range(CHUNKS)]
+        d_scales = [keep.tile([P, CHUNK], U8, name=f"d_scales{c}", align_bytes=64) for c in range(CHUNKS)]
+        banks = [psum.tile([P, PACK, CHUNK], F32, name=f"bank{c}") for c in range(CHUNKS)]
+        y = [keep.tile([P, PACK, CHUNK], F32, name=f"y{c}") for c in range(CHUNKS)]
+        y_in = [keep.tile([P, CHUNK, PACK], BF16, name=f"y_in{c}", align_bytes=64) for c in range(CHUNKS)]
+        y_codes = [keep.tile([P, 2 * CHUNK], U32, name=f"y_codes{h}", align_bytes=64) for h in range(2)]
+        y_scales = keep.tile([P, J], U8, name="y_scales", align_bytes=64)
+        words_out = out_1[0].rearrange("p n t -> p (n t)").bitcast(I32)
+
+        def front(c):
+            j0, j1 = c * CHUNK, (c + 1) * CHUNK
+            gap = subtract(last, f"_c{c}", j0, j1, pick_second(last, f"_c{c}", j0, j1))
+            weigh(last, j0, j1, gap)
+            weave_pair(1, c)
+
+        def product(c):
+            nc.vector.quantize_mx(
+                out=d_codes[c][:].bitcast(E5M2), scales=d_scales[c][:], in_=d_in[c][:].rearrange("p j i -> p (j i)")
+            )
+            for t in range(PACK):
+                nc.tensor.matmul_mx(
+                    out=banks[c][:, t, :],
+                    lhsT=w_dealt[:, t * P : (t + 1) * P].bitcast(E4M3),
+                    lhsT_scale=ws_dealt[:, t * P : (t + 1) * P],
+                    rhs=d_codes[c][:].bitcast(E5M2),
+                    rhs_scale=d_scales[c][:],
+                    start=True,
+                    stop=True,
+                )
+
+        def add_run(c):
+            h, o = divmod(c, 2)
+            nc.vector.tensor_tensor(
+                out=y[c][:], in0=banks[c][:], in1=run_half[h][:, :, o * CHUNK : (o + 1) * CHUNK], op=ALU.add
+            )
+            nc.sync.dma_start(out=out_rows[:, :, c * CHUNK : (c + 1) * CHUNK], in_=y[c][:])
+            nc.scalar.copy(
+                out=y_in[c][:].rearrange("p (a b) t -> p a t b", b=4),
+                in_=y[c][:].rearrange("p t (a b) -> p a t b", b=4),
+            )
+
+        def planes_out(c):
+            h, o = divmod(c, 2)
+            nc.vector.quantize_mx(
+                out=y_codes[h][:, o * CHUNK : (o + 1) * CHUNK].bitcast(E4M3),
+                scales=y_scales[:, c * CHUNK : (c + 1) * CHUNK],
+                in_=y_in[c][:].rearrange("p j t -> p (j t)"),
+            )
+            if o == 1:
+                nc.sync.dma_start(out=words_out[:, h * 2 * CHUNK : (h + 1) * 2 * CHUNK], in_=y_codes[h][:].bitcast(I32))
+
+        stages = [front, product, add_run, planes_out]
+        for step in range(CHUNKS + len(stages) - 1):
+            for s, stage in enumerate(stages):
+                if 0 <= step - s < CHUNKS:
+                    stage(step - s)
+
+        for q in range(4):
+            queue = nc.sync if q % 2 == 0 else nc.scalar
+            queue.dma_start(
+                out=out_2[0, 4 * q : 4 * q + 4, :].bitcast(I32),
+                in_=y_scales[32 * q : 32 * q + 4, :].bitcast(I32),
+            )

@@ -21,7 +21,9 @@ P = 128
 PACK = 4
 CHUNK = 128
 CHUNKS = J // CHUNK
-COLS = CHUNK // 16
+SPANS = [(0, 128), (128, 256), (256, 384), (384, 512)]
+RAMP = [(0, 128), (128, 256), (256, 512)]
+HALVES = [(0, 256), (256, 512)]
 
 
 def tile_list_gradient_of_pair_gaps_pl_kernel(tc, g, rw, w_words, w_scales, run, offs, offs2, out_0, out_1, out_2):
@@ -36,7 +38,6 @@ def tile_list_gradient_of_pair_gaps_pl_kernel(tc, g, rw, w_words, w_scales, run,
         w_raw = keep.tile([P, K], U32, name="w_raw")
         ws_raw = keep.tile([P, K], U8, name="ws_raw")
         w_dealt = keep.tile([P, K], U32, name="w_dealt", align_bytes=64)
-        ws_dealt = keep.tile([P, K], U8, name="ws_dealt", align_bytes=64)
         rw_cols = keep.tile([P, PACK], F32, name="rw_cols")
         ident = keep.tile([P, P], F32, name="ident")
         run_half = [keep.tile([P, PACK, 2 * CHUNK], F32, name=f"run{h}") for h in range(2)]
@@ -45,129 +46,143 @@ def tile_list_gradient_of_pair_gaps_pl_kernel(tc, g, rw, w_words, w_scales, run,
         run_rows = run.rearrange("(p t) j -> p t j", t=PACK)
         out_rows = out_0.rearrange("(p t) j -> p t j", t=PACK)
 
-        nc.sync.dma_start(out=w_raw[:].bitcast(I32), in_=w_words[0].rearrange("p n t -> p (n t)").bitcast(I32))
+        nc.gpsimd.memset(ws_raw[:].bitcast(U32), 0)
+        warm_in = keep.tile([P, 1], F32, name="warm_in")
+        warm = keep.tile([P, 1], F32, name="warm")
+        nc.gpsimd.memset(warm_in[:], 0.0)
+        nc.scalar.activation(warm[:], warm_in[:], COPY)
+        make_identity(nc, ident[:])
         nc.sync.dma_start(out=planes[0][:], in_=g_planes[0])
         nc.sync.dma_start(second[:], offs2)
         nc.sync.dma_start(first[:], offs)
+        nc.sync.dma_start(out=planes[1][:], in_=g_planes[1])
         nc.sync.dma_start(out=rw_cols[:], in_=rw.rearrange("o (k c) -> k (o c)", c=PACK))
-        for i in range(1, PACK):
-            nc.sync.dma_start(out=planes[i][:], in_=g_planes[i])
-        for h in range(2):
-            nc.sync.dma_start(out=run_half[h][:], in_=run_rows[:, :, h * 2 * CHUNK : (h + 1) * 2 * CHUNK])
-
-        nc.vector.memset(ws_raw[:].bitcast(U32), 0)
-        make_identity(nc, ident[:])
+        nc.sync.dma_start(out=planes[2][:], in_=g_planes[2])
         for q in range(4):
-            nc.gpsimd.dma_start(
+            nc.sync.dma_start(
                 out=ws_raw[32 * q : 32 * q + 4, :].bitcast(I32),
                 in_=w_scales[0, 4 * q : 4 * q + 4, :].bitcast(I32),
             )
+        nc.sync.dma_start(out=planes[3][:], in_=g_planes[3])
+        nc.sync.dma_start(out=w_raw[:].bitcast(I32), in_=w_words[0].rearrange("p n t -> p (n t)").bitcast(I32))
+        for h in range(2):
+            nc.sync.dma_start(out=run_half[h][:], in_=run_rows[:, :, h * 2 * CHUNK : (h + 1) * 2 * CHUNK])
 
-        nc.vector.tensor_copy(
-            out=w_dealt[:].rearrange("p (t m) -> p t m", t=PACK),
-            in_=w_raw[:].rearrange("p (m t) -> p t m", t=PACK),
-        )
+        rw_bank = psum.tile([P, P, PACK], F32, name="rw_bank")
+        for c in range(PACK):
+            nc.tensor.transpose(rw_bank[:, :, c], rw_cols[:, c : c + 1].to_broadcast([P, P]), ident[:])
+        rw_all = rw_bank[:].rearrange("p k c -> p (k c)")
+
+        d_in = [keep.tile([P, j1 - j0, PACK], BF16, name=f"d_in{j0}", align_bytes=64) for j0, j1 in SPANS]
+        pairs = [keep.tile([P, 2, j1 - j0, 2], BF16, name=f"pairs{j0}") for j0, j1 in SPANS]
+        gaps_low = [keep.tile([P, 2, j1 - j0], F32, name=f"gaps_low{j0}") for j0, j1 in HALVES]
+        gaps_high = [keep.tile([P, 2, j1 - j0], F32, name=f"gaps_high{j0}") for j0, j1 in SPANS]
+
+        def pick(i, j0, j1):
+            picked = keep.tile([P, j1 - j0], F32, name=f"picked{i}_{j0}", align_bytes=64)
+            nc.scalar.activation(picked[:], planes[i][:].indirect(second[:, j0 // 16 : j1 // 16]), COPY)
+            return picked
+
+        def subtract(i, j0, j1, picked, gap):
+            nc.vector.tensor_tensor(gap, planes[i][:].indirect(first[:, j0 // 16 : j1 // 16]), picked[:], ALU.subtract)
+
+        def weigh(s, u, gap_pair):
+            j0, j1 = SPANS[s]
+            nc.vector.tensor_tensor(
+                out=pairs[s][:, u, :, :],
+                in0=gap_pair.rearrange("p e j -> p j e"),
+                in1=rw_all[:, j0:j1].unsqueeze(2).to_broadcast([P, j1 - j0, 2]),
+                op=ALU.mult,
+            )
+
+        for i in range(2):
+            picked = [pick(i, j0, j1) for j0, j1 in RAMP]
+            for r, (j0, j1) in enumerate(RAMP):
+                h, o = divmod(j0, 2 * CHUNK)
+                subtract(i, j0, j1, picked[r], gaps_low[h][:, i, o : o + j1 - j0])
+                if i == 1 and j1 % (2 * CHUNK) == 0:
+                    for o in range(2):
+                        weigh(2 * h + o, 0, gaps_low[h][:, :, o * CHUNK : (o + 1) * CHUNK])
+        ws_dealt = keep.tile([P, K], U8, name="ws_dealt", tag="picked1_256", align_bytes=64)
         nc.vector.tensor_copy(
             out=ws_dealt[:].rearrange("p (t m) -> p t m", t=PACK),
             in_=ws_raw[:].rearrange("p (m t) -> p t m", t=PACK),
         )
+        picked = [pick(2, j0, j1) for j0, j1 in SPANS]
+        for s, (j0, j1) in enumerate(SPANS):
+            subtract(2, j0, j1, picked[s], gaps_high[s][:, 0, :])
 
-        rw_bank = psum.tile([P, PACK, P], F32, name="rw_bank")
-        for c in range(PACK):
-            nc.tensor.transpose(rw_bank[:, c, :], rw_cols[:, c : c + 1].to_broadcast([P, P]), ident[:])
-        rw_all = rw_bank[:].rearrange("p c k -> p k c")
-
-        pairs = [keep.tile([P, 2, J], BF16, name=f"pair{u}") for u in range(2)]
-        d_in = [keep.tile([P, CHUNK, PACK], BF16, name=f"d_in{c}", align_bytes=64) for c in range(CHUNKS)]
-
-        def pick_second(i, tag, j0, j1):
-            picked = keep.tile([P, j1 - j0], F32, name=f"picked{tag}")
-            nc.scalar.activation(picked[:], planes[i][:].indirect(second[:, j0 // 16 : j1 // 16]), COPY)
-            return picked
-
-        def subtract(i, tag, j0, j1, picked):
-            gap = keep.tile([P, j1 - j0], F32, name=f"gap{tag}")
-            nc.vector.tensor_tensor(gap[:], planes[i][:].indirect(first[:, j0 // 16 : j1 // 16]), picked[:], ALU.subtract)
-            return gap
-
-        def weigh(i, j0, j1, gap):
-            nc.vector.tensor_tensor(
-                out=pairs[i // 2][:, i % 2, j0:j1].rearrange("p (k c) -> p k c", c=PACK),
-                in0=gap[:].rearrange("p (k c) -> p k c", c=PACK),
-                in1=rw_all[:, j0 // PACK : j1 // PACK, :],
-                op=ALU.mult,
-            )
-
-        def weave_pair(u, c):
-            nc.scalar.copy(
-                out=d_in[c][:, :, 2 * u : 2 * u + 2],
-                in_=pairs[u][:, :, c * CHUNK : (c + 1) * CHUNK].rearrange("p e j -> p j e"),
-            )
-
-        for i in range(PACK - 1):
-            gap = subtract(i, f"_{i}", 0, J, pick_second(i, f"_{i}", 0, J))
-            weigh(i, 0, J, gap)
-            if i == 1:
-                for c in range(CHUNKS):
-                    weave_pair(0, c)
-
-        last = PACK - 1
-        d_codes = [keep.tile([P, CHUNK], U32, name=f"d_codes{c}", align_bytes=64) for c in range(CHUNKS)]
-        d_scales = [keep.tile([P, CHUNK], U8, name=f"d_scales{c}", align_bytes=64) for c in range(CHUNKS)]
+        d_codes = [keep.tile([P, j1 - j0], U32, name=f"d_codes{j0}", align_bytes=64) for j0, j1 in SPANS]
+        d_scales = [keep.tile([P, j1 - j0], U8, name=f"d_scales{j0}", align_bytes=64) for j0, j1 in SPANS]
         banks = [psum.tile([P, PACK, CHUNK], F32, name=f"bank{c}") for c in range(CHUNKS)]
         y = [keep.tile([P, PACK, CHUNK], F32, name=f"y{c}") for c in range(CHUNKS)]
-        y_in = [keep.tile([P, CHUNK, PACK], BF16, name=f"y_in{c}", align_bytes=64) for c in range(CHUNKS)]
-        y_codes = [keep.tile([P, 2 * CHUNK], U32, name=f"y_codes{h}", align_bytes=64) for h in range(2)]
+        y_spans = [(0, J - CHUNK), (J - CHUNK, J)]
+        y_in = [keep.tile([P, j1 - j0, PACK], BF16, name=f"y_in{j0}", align_bytes=64) for j0, j1 in y_spans]
+        y_codes = [keep.tile([P, j1 - j0], U32, name=f"y_codes{j0}", align_bytes=64) for j0, j1 in y_spans]
         y_scales = keep.tile([P, J], U8, name="y_scales", align_bytes=64)
         words_out = out_1[0].rearrange("p n t -> p (n t)").bitcast(I32)
 
-        def front(c):
-            j0, j1 = c * CHUNK, (c + 1) * CHUNK
-            gap = subtract(last, f"_c{c}", j0, j1, pick_second(last, f"_c{c}", j0, j1))
-            weigh(last, j0, j1, gap)
-            weave_pair(1, c)
+        picked = [pick(3, j0, j1) for j0, j1 in SPANS]
 
-        def product(c):
-            nc.vector.quantize_mx(
-                out=d_codes[c][:].bitcast(E5M2), scales=d_scales[c][:], in_=d_in[c][:].rearrange("p j i -> p (j i)")
+        def gap_last(s):
+            subtract(3, SPANS[s][0], SPANS[s][1], picked[s], gaps_high[s][:, 1, :])
+
+        def weigh_weave(s):
+            weigh(s, 1, gaps_high[s][:])
+            nc.scalar.copy(
+                out=d_in[s][:].rearrange("p j i -> p (j i)").bitcast(U32).rearrange("p (j u) -> p j u", u=2),
+                in_=pairs[s][:].rearrange("p u j e -> p (u j e)").bitcast(U32).rearrange("p (u j) -> p j u", u=2),
             )
-            for t in range(PACK):
-                nc.tensor.matmul_mx(
-                    out=banks[c][:, t, :],
-                    lhsT=w_dealt[:, t * P : (t + 1) * P].bitcast(E4M3),
-                    lhsT_scale=ws_dealt[:, t * P : (t + 1) * P],
-                    rhs=d_codes[c][:].bitcast(E5M2),
-                    rhs_scale=d_scales[c][:],
-                    start=True,
-                    stop=True,
-                )
+
+        def deal_words():
+            nc.scalar.copy(
+                out=w_dealt[:].rearrange("p (t m) -> p m t", t=PACK),
+                in_=w_raw[:].rearrange("p (m t) -> p m t", t=PACK),
+            )
+
+        def product(s):
+            j0, j1 = SPANS[s]
+            nc.vector.quantize_mx(
+                out=d_codes[s][:].bitcast(E5M2), scales=d_scales[s][:], in_=d_in[s][:].rearrange("p j i -> p (j i)")
+            )
+            for o in range(0, j1 - j0, CHUNK):
+                for t in range(PACK):
+                    nc.tensor.matmul_mx(
+                        out=banks[(j0 + o) // CHUNK][:, t, :],
+                        lhsT=w_dealt[:, t * P : (t + 1) * P].bitcast(E4M3),
+                        lhsT_scale=ws_dealt[:, t * P : (t + 1) * P],
+                        rhs=d_codes[s][:, o : o + CHUNK].bitcast(E5M2),
+                        rhs_scale=d_scales[s][:, o : o + CHUNK],
+                        start=True,
+                        stop=True,
+                    )
 
         def add_run(c):
             h, o = divmod(c, 2)
-            nc.vector.tensor_tensor(
-                out=y[c][:], in0=banks[c][:], in1=run_half[h][:, :, o * CHUNK : (o + 1) * CHUNK], op=ALU.add
-            )
+            cols = slice(o * CHUNK, (o + 1) * CHUNK)
+            nc.vector.tensor_tensor(out=y[c][:], in0=banks[c][:], in1=run_half[h][:, :, cols], op=ALU.add)
             nc.sync.dma_start(out=out_rows[:, :, c * CHUNK : (c + 1) * CHUNK], in_=y[c][:])
+            u, o = divmod(c, CHUNKS - 1)
             nc.scalar.copy(
-                out=y_in[c][:].rearrange("p (a b) t -> p a t b", b=4),
+                out=y_in[u][:, o * CHUNK : (o + 1) * CHUNK, :].rearrange("p (a b) t -> p a t b", b=4),
                 in_=y[c][:].rearrange("p t (a b) -> p a t b", b=4),
             )
 
-        def planes_out(c):
-            h, o = divmod(c, 2)
-            nc.vector.quantize_mx(
-                out=y_codes[h][:, o * CHUNK : (o + 1) * CHUNK].bitcast(E4M3),
-                scales=y_scales[:, c * CHUNK : (c + 1) * CHUNK],
-                in_=y_in[c][:].rearrange("p j t -> p (j t)"),
-            )
-            if o == 1:
-                nc.sync.dma_start(out=words_out[:, h * 2 * CHUNK : (h + 1) * 2 * CHUNK], in_=y_codes[h][:].bitcast(I32))
+        stages = [(gap_last, 0), (product, 3), (weigh_weave, 1), (add_run, 5)]
+        for step in range(CHUNKS + 5):
+            for stage, lag in stages:
+                if 0 <= step - lag < CHUNKS:
+                    stage(step - lag)
+            if step == 1:
+                deal_words()
 
-        stages = [front, product, add_run, planes_out]
-        for step in range(CHUNKS + len(stages) - 1):
-            for s, stage in enumerate(stages):
-                if 0 <= step - s < CHUNKS:
-                    stage(step - s)
+        for u, (j0, j1) in enumerate(y_spans):
+            nc.vector.quantize_mx(
+                out=y_codes[u][:].bitcast(E4M3),
+                scales=y_scales[:, j0:j1],
+                in_=y_in[u][:].rearrange("p j t -> p (j t)"),
+            )
+            nc.sync.dma_start(out=words_out[:, j0:j1], in_=y_codes[u][:].bitcast(I32))
 
         for q in range(4):
             queue = nc.sync if q % 2 == 0 else nc.scalar

@@ -89,9 +89,9 @@ def tile_list_gradient_of_pair_gaps_pl_kernel(tc, g, rw, w_words, w_scales, run,
         def weigh(s, u, gap_pair):
             j0, j1 = SPANS[s]
             nc.vector.tensor_tensor(
-                out=pairs[s][:, u, :, :],
-                in0=gap_pair.rearrange("p e j -> p j e"),
-                in1=rw_all[:, j0:j1].unsqueeze(2).to_broadcast([P, j1 - j0, 2]),
+                out=pairs[s][:, u, :, :].rearrange("p (a b) e -> p a e b", b=4),
+                in0=gap_pair.rearrange("p e (a b) -> p a e b", b=4),
+                in1=rw_all[:, j0:j1].rearrange("p (a b) -> p a b", b=4).unsqueeze(2).to_broadcast([P, (j1 - j0) // 4, 2, 4]),
                 op=ALU.mult,
             )
 
@@ -164,8 +164,8 @@ def tile_list_gradient_of_pair_gaps_pl_kernel(tc, g, rw, w_words, w_scales, run,
             nc.sync.dma_start(out=out_rows[:, :, c * CHUNK : (c + 1) * CHUNK], in_=y[c][:])
             u, o = divmod(c, CHUNKS - 1)
             nc.scalar.copy(
-                out=y_in[u][:, o * CHUNK : (o + 1) * CHUNK, :].rearrange("p (a b) t -> p a t b", b=4),
-                in_=y[c][:].rearrange("p t (a b) -> p a t b", b=4),
+                out=y_in[u][:, o * CHUNK : (o + 1) * CHUNK, :].rearrange("p (a b) t -> p a t b", b=2),
+                in_=y[c][:].rearrange("p t (a b) -> p a t b", b=2),
             )
 
         stages = [(gap_last, 0), (product, 3), (weigh_weave, 1), (add_run, 5)]

from contextlib import ExitStack

import concourse.mybir as mybir
from concourse.masks import make_identity

N, K, T, J = 512, 512, 2048, 512
FLOPS = 2 * N * K * J

F32 = mybir.dt.float32
BF16 = mybir.dt.bfloat16
I32 = mybir.dt.int32
U32 = mybir.dt.uint32
U16 = mybir.dt.uint16
U8 = mybir.dt.uint8
E4M3 = mybir.dt.float8_e4m3fn_x4
E5M2 = mybir.dt.float8_e5m2_x4
ALU = mybir.AluOpType
COPY = mybir.ActivationFunctionType.Copy

P = 128
PACK = 4
CHUNK = 128
CHUNKS = J // CHUNK
SPANS = [(0, 128), (128, 256), (256, 384), (384, 512)]
RAMP = [(0, 128), (128, 256), (256, 512)]
HALVES = [(0, 256), (256, 512)]


def tile_list_gradient_of_pair_gaps_pl_kernel(tc, g, rw, w_words, w_scales, run, offs, offs2, out_0, out_1, out_2):
    nc = tc.nc
    with ExitStack() as ctx:
        keep = ctx.enter_context(tc.tile_pool(name="keep", bufs=1))
        psum = ctx.enter_context(tc.psum_pool(name="psum", bufs=1))

        first = keep.tile([P, J // 16], U16, name="first")
        second = keep.tile([P, J // 16], U16, name="second")
        planes = [keep.tile([P, T], F32, name=f"g{i}") for i in range(PACK)]
        w_raw = keep.tile([P, K], U32, name="w_raw")
        ws_raw = keep.tile([P, K], U8, name="ws_raw")
        w_dealt = keep.tile([P, K], U32, name="w_dealt", align_bytes=64)
        rw_cols = keep.tile([P, PACK], F32, name="rw_cols")
        ident = keep.tile([P, P], F32, name="ident")
        run_half = [keep.tile([P, PACK, 2 * CHUNK], F32, name=f"run{h}") for h in range(2)]

        g_planes = g.rearrange("(p i) t -> i p t", i=PACK)
        run_rows = run.rearrange("(p t) j -> p t j", t=PACK)
        out_rows = out_0.rearrange("(p t) j -> p t j", t=PACK)

        nc.gpsimd.memset(ws_raw[:].bitcast(U32), 0)
        warm_in = keep.tile([P, 1], F32, name="warm_in")
        warm = keep.tile([P, 1], F32, name="warm")
        nc.gpsimd.memset(warm_in[:], 0.0)
        nc.scalar.activation(warm[:], warm_in[:], COPY)
        make_identity(nc, ident[:])
        nc.sync.dma_start(out=planes[0][:], in_=g_planes[0])
        nc.sync.dma_start(second[:], offs2)
        nc.sync.dma_start(first[:], offs)
        nc.sync.dma_start(out=planes[1][:], in_=g_planes[1])
        nc.sync.dma_start(out=rw_cols[:], in_=rw.rearrange("o (k c) -> k (o c)", c=PACK))
        nc.sync.dma_start(out=planes[2][:], in_=g_planes[2])
        for q in range(4):
            nc.sync.dma_start(
                out=ws_raw[32 * q : 32 * q + 4, :].bitcast(I32),
                in_=w_scales[0, 4 * q : 4 * q + 4, :].bitcast(I32),
            )
        nc.sync.dma_start(out=planes[3][:], in_=g_planes[3])
        nc.sync.dma_start(out=w_raw[:].bitcast(I32), in_=w_words[0].rearrange("p n t -> p (n t)").bitcast(I32))
        for h in range(2):
            nc.sync.dma_start(out=run_half[h][:], in_=run_rows[:, :, h * 2 * CHUNK : (h + 1) * 2 * CHUNK])

        rw_bank = psum.tile([P, P, PACK], F32, name="rw_bank")
        for c in range(PACK):
            nc.tensor.transpose(rw_bank[:, :, c], rw_cols[:, c : c + 1].to_broadcast([P, P]), ident[:])
        rw_all = rw_bank[:].rearrange("p k c -> p (k c)")

        d_in = [keep.tile([P, j1 - j0, PACK], BF16, name=f"d_in{j0}", align_bytes=64) for j0, j1 in SPANS]
        pairs = [keep.tile([P, 2, j1 - j0, 2], BF16, name=f"pairs{j0}") for j0, j1 in SPANS]
        gaps_low = [keep.tile([P, 2, j1 - j0], F32, name=f"gaps_low{j0}") for j0, j1 in HALVES]
        gaps_high = [keep.tile([P, 2, j1 - j0], F32, name=f"gaps_high{j0}") for j0, j1 in SPANS]

        def pick(i, j0, j1):
            picked = keep.tile([P, j1 - j0], F32, name=f"picked{i}_{j0}", align_bytes=64)
            nc.scalar.activation(picked[:], planes[i][:].indirect(second[:, j0 // 16 : j1 // 16]), COPY)
            return picked

        def subtract(i, j0, j1, picked, gap):
            nc.vector.tensor_tensor(gap, planes[i][:].indirect(first[:, j0 // 16 : j1 // 16]), picked[:], ALU.subtract)

        def weigh(s, u, gap_pair):
            j0, j1 = SPANS[s]
            nc.vector.tensor_tensor(
                out=pairs[s][:, u, :, :].rearrange("p (a b) e -> p a e b", b=4),
                in0=gap_pair.rearrange("p e (a b) -> p a e b", b=4),
                in1=rw_all[:, j0:j1].rearrange("p (a b) -> p a b", b=4).unsqueeze(2).to_broadcast([P, (j1 - j0) // 4, 2, 4]),
                op=ALU.mult,
            )

        for i in range(2):
            picked = [pick(i, j0, j1) for j0, j1 in RAMP]
            for r, (j0, j1) in enumerate(RAMP):
                h, o = divmod(j0, 2 * CHUNK)
                subtract(i, j0, j1, picked[r], gaps_low[h][:, i, o : o + j1 - j0])
                if i == 1 and j1 % (2 * CHUNK) == 0:
                    for o in range(2):
                        weigh(2 * h + o, 0, gaps_low[h][:, :, o * CHUNK : (o + 1) * CHUNK])
        ws_dealt = keep.tile([P, K], U8, name="ws_dealt", tag="picked1_256", align_bytes=64)
        nc.vector.tensor_copy(
            out=ws_dealt[:].rearrange("p (t m) -> p t m", t=PACK),
            in_=ws_raw[:].rearrange("p (m t) -> p t m", t=PACK),
        )
        picked = [pick(2, j0, j1) for j0, j1 in SPANS]
        for s, (j0, j1) in enumerate(SPANS):
            subtract(2, j0, j1, picked[s], gaps_high[s][:, 0, :])

        d_codes = [keep.tile([P, j1 - j0], U32, name=f"d_codes{j0}", align_bytes=64) for j0, j1 in SPANS]
        d_scales = [keep.tile([P, j1 - j0], U8, name=f"d_scales{j0}", align_bytes=64) for j0, j1 in SPANS]
        banks = [psum.tile([P, PACK, CHUNK], F32, name=f"bank{c}") for c in range(CHUNKS)]
        y = [keep.tile([P, PACK, CHUNK], F32, name=f"y{c}") for c in range(CHUNKS)]
        y_spans = [(0, J - CHUNK), (J - CHUNK, J)]
        y_in = [keep.tile([P, j1 - j0, PACK], BF16, name=f"y_in{j0}", align_bytes=64) for j0, j1 in y_spans]
        y_codes = [keep.tile([P, j1 - j0], U32, name=f"y_codes{j0}", align_bytes=64) for j0, j1 in y_spans]
        y_scales = keep.tile([P, J], U8, name="y_scales", align_bytes=64)
        words_out = out_1[0].rearrange("p n t -> p (n t)").bitcast(I32)

        picked = [pick(3, j0, j1) for j0, j1 in SPANS]

        def gap_last(s):
            subtract(3, SPANS[s][0], SPANS[s][1], picked[s], gaps_high[s][:, 1, :])

        def weigh_weave(s):
            weigh(s, 1, gaps_high[s][:])
            nc.scalar.copy(
                out=d_in[s][:].rearrange("p j i -> p (j i)").bitcast(U32).rearrange("p (j u) -> p j u", u=2),
                in_=pairs[s][:].rearrange("p u j e -> p (u j e)").bitcast(U32).rearrange("p (u j) -> p j u", u=2),
            )

        def deal_words():
            nc.scalar.copy(
                out=w_dealt[:].rearrange("p (t m) -> p m t", t=PACK),
                in_=w_raw[:].rearrange("p (m t) -> p m t", t=PACK),
            )

        def product(s):
            j0, j1 = SPANS[s]
            nc.vector.quantize_mx(
                out=d_codes[s][:].bitcast(E5M2), scales=d_scales[s][:], in_=d_in[s][:].rearrange("p j i -> p (j i)")
            )
            for o in range(0, j1 - j0, CHUNK):
                for t in range(PACK):
                    nc.tensor.matmul_mx(
                        out=banks[(j0 + o) // CHUNK][:, t, :],
                        lhsT=w_dealt[:, t * P : (t + 1) * P].bitcast(E4M3),
                        lhsT_scale=ws_dealt[:, t * P : (t + 1) * P],
                        rhs=d_codes[s][:, o : o + CHUNK].bitcast(E5M2),
                        rhs_scale=d_scales[s][:, o : o + CHUNK],
                        start=True,
                        stop=True,
                    )

        def add_run(c):
            h, o = divmod(c, 2)
            cols = slice(o * CHUNK, (o + 1) * CHUNK)
            nc.vector.tensor_tensor(out=y[c][:], in0=banks[c][:], in1=run_half[h][:, :, cols], op=ALU.add)
            nc.sync.dma_start(out=out_rows[:, :, c * CHUNK : (c + 1) * CHUNK], in_=y[c][:])
            u, o = divmod(c, CHUNKS - 1)
            nc.scalar.copy(
                out=y_in[u][:, o * CHUNK : (o + 1) * CHUNK, :].rearrange("p (a b) t -> p a t b", b=2),
                in_=y[c][:].rearrange("p t (a b) -> p a t b", b=2),
            )

        stages = [(gap_last, 0), (product, 3), (weigh_weave, 1), (add_run, 5)]
        for step in range(CHUNKS + 5):
            for stage, lag in stages:
                if 0 <= step - lag < CHUNKS:
                    stage(step - lag)
            if step == 1:
                deal_words()

        for u, (j0, j1) in enumerate(y_spans):
            nc.vector.quantize_mx(
                out=y_codes[u][:].bitcast(E4M3),
                scales=y_scales[:, j0:j1],
                in_=y_in[u][:].rearrange("p j t -> p (j t)"),
            )
            nc.sync.dma_start(out=words_out[:, j0:j1], in_=y_codes[u][:].bitcast(I32))

        for q in range(4):
            queue = nc.sync if q % 2 == 0 else nc.scalar
            queue.dma_start(
                out=out_2[0, 4 * q : 4 * q + 4, :].bitcast(I32),
                in_=y_scales[32 * q : 32 * q + 4, :].bitcast(I32),
            )
